import numpy as np
import ml_dtypes


def mxq(x, axis, fmt="e4m3"):
    dtype, down = {"e4m3": (ml_dtypes.float8_e4m3fn, 7), "e5m2": (ml_dtypes.float8_e5m2, 14)}[fmt]
    v = np.moveaxis(np.asarray(x, np.float32).astype(ml_dtypes.bfloat16).astype(np.float64), axis, -1)
    blocks = v.reshape(v.shape[:-1] + (-1, 32))
    amax = np.abs(blocks).max(-1, keepdims=True)
    byte = np.maximum(np.where(amax > 0, np.frexp(amax)[1] - 1 + 127, 0) - down, 1)
    scale = np.exp2(byte - 127.0)
    codes = (blocks / scale).astype(np.float32).astype(dtype).astype(np.float64)
    return np.moveaxis((codes * scale).reshape(v.shape), -1, axis)


WIDE = False


def mx_kscale(k):
    if not WIDE:
        return np.ones(k)
    levels = np.array([10, -10, 5, -5, 0])
    if k % 512:
        return np.exp2(np.random.permutation(np.resize(levels, k // 32))).repeat(32)
    a = np.empty((k // 512, 16))
    for p in range(k // 512):
        a[p, :8] = np.random.permutation(np.resize(levels, 8))
        for g in range(8):
            far = levels[np.abs(levels - a[p, g]) >= 10]
            a[p, g + 8] = far[np.random.randint(len(far))]
    return np.exp2(a.ravel()).repeat(32)


def f64(x):
    return np.asarray(x).astype(np.float64)


def striped(idx):
    return np.tile(np.asarray(idx).reshape(-1, 16).T, (8, 1)).astype(np.uint16)


def unstriped(offs):
    return offs[:16].T.reshape(-1).astype(np.int64)


E2M1 = np.array([0.0, 0.5, 1.0, 1.5, 2.0, 3.0, 4.0, 6.0, -0.0, -0.5, -1.0, -1.5, -2.0, -3.0, -4.0, -6.0])


def pack_weight(w, fmt):
    k, n = w.shape
    w = f64(np.asarray(w, np.float32).astype(ml_dtypes.bfloat16)).reshape(k // 32, 32, n)
    amax = np.abs(w).max(1)
    if fmt == "e4m3":
        byte = np.frexp(amax)[1] - 1 + 127 - 7
    else:
        mant, ex = np.frexp(amax / 6.0)
        byte = np.where(mant > 0.5, ex, ex - 1) + 127
    byte = np.clip(np.where(amax > 0, byte, 1), 1, 254)
    scaled = (w * np.exp2(127.0 - byte)[:, None, :]).reshape(k, n).astype(np.float32)
    by_word = np.ascontiguousarray(scaled.reshape(k // 512, 128, 4, n).transpose(0, 1, 3, 2))
    if fmt == "e4m3":
        words = by_word.astype(ml_dtypes.float8_e4m3fn).view(np.uint8)
    else:
        c = by_word.astype(ml_dtypes.float4_e2m1fn).view(np.uint8) & 0xF
        words = (c[..., 0::2] | (c[..., 1::2] << 4)).reshape(k // 512, 128, 2 * n)
    return np.ascontiguousarray(words), np.ascontiguousarray(byte.astype(np.uint8).reshape(k // 512, 16, n))


def unpack_weight(words, scales, fmt):
    g, _, n = scales.shape
    words = np.ascontiguousarray(words).reshape(g, 128, n, -1)
    if fmt == "e4m3":
        vals = words.view(ml_dtypes.float8_e4m3fn).astype(np.float64)
    else:
        nib = np.empty((g, 128, n, 4), np.uint8)
        nib[..., 0::2] = words & 0xF
        nib[..., 1::2] = words >> 4
        vals = E2M1[nib]
    vals = vals * np.repeat(np.exp2(scales.astype(np.float64) - 127.0), 8, axis=1)[..., None]
    return vals.transpose(0, 1, 3, 2).reshape(g * 512, n)


D, T, U, I, J = 512, 1024, 1024, 256, 512


def setup_inputs():
    n = np.random.standard_normal
    idx = np.random.permutation(T)[:I]
    idx2 = np.random.permutation(U)[:J]
    fd = mx_kscale(D)
    tabbp = pack_weight(n((D, U)) / fd[:, None], "e4m3")
    return {
        "taba": (n((D, T)) * 1 / np.sqrt(D) * fd[:, None]).astype(np.float32),
        "tabb_words": tabbp[0],
        "tabb_scales": tabbp[1],
        "cost": (n((I, J)) * 1.0).astype(np.float32),
        "greed": (np.random.uniform(0.3, 1.2, (I, 1))).astype(np.float32),
        "old": (0.3 * n((I, J))).astype(np.float32),
        "offs": striped(idx),
        "offs2": striped(idx2),
    }


def reference(taba, tabb_words, tabb_scales, cost, greed, old, offs, offs2):
    idx = unstriped(offs)
    idx2 = unstriped(offs2)
    tabbu = unpack_weight(tabb_words, tabb_scales, "e4m3")
    tabaidxq = mxq(f64(taba)[:, idx], 0, "e4m3")
    tabbidx2g = tabbu[:, idx2]
    s = tabaidxq.T @ tabbidx2g
    b = s - np.max(s, axis=1, keepdims=True)
    p = np.exp(b)
    z = np.sum(p, axis=1, keepdims=True)
    dz = f64(greed) * (-1.0) / z - np.sum(p * f64(cost), axis=1, keepdims=True) / np.square(z) - f64(greed) * np.sum(p * b, axis=1, keepdims=True) / np.square(z)
    dp = 1.0 / z * f64(cost) + f64(greed) / z * b + dz
    db = f64(greed) / z * p + dp * p
    y = db * 256.0 + f64(old)
    return y

@@ -1,0 +1,104 @@
+from contextlib import ExitStack
+
+import concourse.mybir as mybir
+
+D, T, U, I, J = 512, 1024, 1024, 256, 512
+FLOPS = 2 * D * I * J
+
+F32 = mybir.dt.float32
+BF16 = mybir.dt.bfloat16
+I32 = mybir.dt.int32
+U32 = mybir.dt.uint32
+U16 = mybir.dt.uint16
+U8 = mybir.dt.uint8
+FP8X4 = mybir.dt.float8_e4m3fn_x4
+ALU = mybir.AluOpType
+ACT = mybir.ActivationFunctionType
+AX = mybir.AxisListType
+
+P = 128
+PACK = 4
+TILES = I // P
+LIST_COLS = P // 16
+GAIN = 256.0
+
+
+def tile_attend_bpaircost_kernel(tc, taba, tabb_words, tabb_scales, cost, greed, old, offs, offs2, out):
+    nc = tc.nc
+    with ExitStack() as ctx:
+        sb = ctx.enter_context(tc.tile_pool(name="sb", bufs=1))
+        ps = ctx.enter_context(tc.psum_pool(name="ps", bufs=1))
+
+        offs_t = sb.tile([P, I // 16], U16, name="offs_t")
+        offs2_t = sb.tile([P, J // 16], U16, name="offs2_t")
+        b_words = sb.tile([P, U], U32, name="b_words", align_bytes=64)
+        b_bytes = sb.tile([P, U], U8, name="b_bytes", align_bytes=64)
+        planes = [sb.tile([P, T], F32, name=f"plane{r}", align_bytes=64) for r in range(PACK)]
+        greed_t = sb.tile([P, TILES], F32, name="greed_t")
+        cost_t = [sb.tile([P, J], F32, name=f"cost{t}") for t in range(TILES)]
+        old_t = [sb.tile([P, J], F32, name=f"old{t}") for t in range(TILES)]
+
+        nc.vector.memset(b_bytes[:].bitcast(I32), 0)
+        nc.sync.dma_start(b_words[:].bitcast(I32), tabb_words[0].rearrange("p c r -> p (c r)").bitcast(I32))
+        nc.sync.dma_start(offs2_t[:], offs2)
+        nc.sync.dma_start(offs_t[:], offs)
+        for q in range(4):
+            nc.scalar.dma_start(b_bytes[32 * q : 32 * q + 4, :].bitcast(I32), tabb_scales[0, 4 * q : 4 * q + 4, :].bitcast(I32))
+        rows = taba.rearrange("(p r) c -> p r c", r=PACK)
+        for r in range(PACK):
+            nc.sync.dma_start(planes[r][:], rows[:, r, :])
+        with nc.allow_non_contiguous_dma(reason="one greed value for each row"):
+            nc.sync.dma_start(greed_t[:], greed.rearrange("(t p) o -> p (t o)", p=P))
+        for t in range(TILES):
+            nc.sync.dma_start(cost_t[t][:], cost[t * P : (t + 1) * P, :])
+        for t in range(TILES):
+            nc.sync.dma_start(old_t[t][:], old[t * P : (t + 1) * P, :])
+
+        g_words = sb.tile([P, J], U32, name="g_words", align_bytes=64)
+        g_bytes = sb.tile([P, J], U8, name="g_bytes", align_bytes=64)
+        nc.vector.tensor_copy(g_words[:], b_words[:].indirect(offs2_t[:]))
+        nc.vector.tensor_copy(g_bytes[:], b_bytes[:].indirect(offs2_t[:]))
+
+        a_bf = [sb.tile([P, P, PACK], BF16, name=f"a_bf{t}", align_bytes=64) for t in range(TILES)]
+        a_words = [sb.tile([P, P], U32, name=f"a_words{t}", align_bytes=64) for t in range(TILES)]
+        a_bytes = [sb.tile([P, P], U8, name=f"a_bytes{t}", align_bytes=64) for t in range(TILES)]
+        for r in range(PACK):
+            for t in range(TILES):
+                nc.vector.tensor_copy(a_bf[t][:, :, r], planes[r][:].indirect(offs_t[:, t * LIST_COLS : (t + 1) * LIST_COLS]))
+        neg_greed = sb.tile([P, TILES], F32, name="neg_greed")
+        nc.gpsimd.tensor_scalar(neg_greed[:], greed_t[:], -1.0, 0.0, ALU.mult, ALU.add)
+        scores = [ps.tile([P, J], F32, name=f"scores{t}") for t in range(TILES)]
+        for t in range(TILES):
+            nc.vector.quantize_mx(out=a_words[t][:].bitcast(FP8X4), scales=a_bytes[t][:], in_=a_bf[t][:].rearrange("p c r -> p (c r)"))
+        for t in range(TILES):
+            nc.tensor.matmul_mx(out=scores[t][:], lhsT=a_words[t][:].bitcast(FP8X4), lhsT_scale=a_bytes[t][:],
+                                rhs=g_words[:].bitcast(FP8X4), rhs_scale=g_bytes[:], start=True, stop=True)
+
+        neg_max = [sb.tile([P, 1], F32, name=f"neg_max{t}") for t in range(TILES)]
+        z = sb.tile([P, TILES], F32, name="z")
+        rz = sb.tile([P, TILES], F32, name="rz")
+        neg_k = sb.tile([P, TILES], F32, name="neg_k")
+        k_rz = sb.tile([P, TILES], F32, name="k_rz")
+        p = [sb.tile([P, J], F32, name=f"p{t}") for t in range(TILES)]
+        neg_w = [sb.tile([P, J], F32, name=f"neg_w{t}") for t in range(TILES)]
+        neg_pw = [sb.tile([P, J], F32, name=f"neg_pw{t}") for t in range(TILES)]
+        neg_sum = [sb.tile([P, 1], F32, name=f"neg_sum{t}") for t in range(TILES)]
+        p_gain = [sb.tile([P, 1], F32, name=f"p_gain{t}") for t in range(TILES)]
+        part = [sb.tile([P, J], F32, name=f"part{t}") for t in range(TILES)]
+        res = [sb.tile([P, J], F32, name=f"res{t}") for t in range(TILES)]
+
+        for t in range(TILES):
+            nc.vector.tensor_reduce(neg_max[t][:], scores[t][:], AX.X, ALU.max, negate=True)
+        for t in range(TILES):
+            nc.scalar.activation(p[t][:], scores[t][:], ACT.Exp, bias=neg_max[t][:], scale=1.0, accum_out=z[:, t : t + 1])
+        for t in range(TILES):
+            nc.vector.scalar_tensor_tensor(neg_w[t][:], scores[t][:], neg_greed[:, t : t + 1], cost_t[t][:], ALU.mult, ALU.subtract)
+        nc.vector.reciprocal(rz[:], z[:])
+        nc.scalar.activation(neg_k[:], rz[:], ACT.Copy, scale=-GAIN)
+        nc.scalar.activation(k_rz[:], rz[:], ACT.Square, scale=16.0)
+        for t in range(TILES):
+            nc.vector.scalar_tensor_tensor(neg_pw[t][:], p[t][:], 1.0, neg_w[t][:], ALU.mult, ALU.mult, accum_out=neg_sum[t][:])
+            nc.scalar.activation(p_gain[t][:], neg_sum[t][:], ACT.Copy, scale=k_rz[:, t : t + 1])
+            nc.vector.scalar_tensor_tensor(part[t][:], neg_pw[t][:], neg_k[:, t : t + 1], old_t[t][:], ALU.mult, ALU.add)
+            nc.vector.scalar_tensor_tensor(res[t][:], p[t][:], p_gain[t][:], part[t][:], ALU.mult, ALU.add)
+            nc.sync.dma_start(out[t * P : (t + 1) * P, :], res[t][:])

@@ -38,14 +38,15 @@ def tile_attend_bpaircost_kernel(tc, taba, tabb_words, tabb_scales, cost, greed,
         cost_t = [sb.tile([P, J], F32, name=f"cost{t}") for t in range(TILES)]
         old_t = [sb.tile([P, J], F32, name=f"old{t}") for t in range(TILES)]
 
-        nc.vector.memset(b_bytes[:].bitcast(I32), 0)
-        nc.sync.dma_start(b_words[:].bitcast(I32), tabb_words[0].rearrange("p c r -> p (c r)").bitcast(I32))
-        nc.sync.dma_start(offs2_t[:], offs2)
-        nc.sync.dma_start(offs_t[:], offs)
-        for q in range(4):
-            nc.scalar.dma_start(b_bytes[32 * q : 32 * q + 4, :].bitcast(I32), tabb_scales[0, 4 * q : 4 * q + 4, :].bitcast(I32))
         rows = taba.rearrange("(p r) c -> p r c", r=PACK)
-        for r in range(PACK):
+        nc.vector.memset(b_bytes[:].bitcast(I32), 0)
+        nc.sync.dma_start(offs_t[:], offs)
+        nc.sync.dma_start(planes[0][:], rows[:, 0, :])
+        nc.sync.dma_start(offs2_t[:], offs2)
+        nc.sync.dma_start(b_words[:].bitcast(I32), tabb_words[0].rearrange("p c r -> p (c r)").bitcast(I32))
+        for q in range(4):
+            nc.sync.dma_start(b_bytes[32 * q : 32 * q + 4, :].bitcast(I32), tabb_scales[0, 4 * q : 4 * q + 4, :].bitcast(I32))
+        for r in range(1, PACK):
             nc.sync.dma_start(planes[r][:], rows[:, r, :])
         with nc.allow_non_contiguous_dma(reason="one greed value for each row"):
             nc.sync.dma_start(greed_t[:], greed.rearrange("(t p) o -> p (t o)", p=P))
@@ -62,11 +63,14 @@ def tile_attend_bpaircost_kernel(tc, taba, tabb_words, tabb_scales, cost, greed,
         a_bf = [sb.tile([P, P, PACK], BF16, name=f"a_bf{t}", align_bytes=64) for t in range(TILES)]
         a_words = [sb.tile([P, P], U32, name=f"a_words{t}", align_bytes=64) for t in range(TILES)]
         a_bytes = [sb.tile([P, P], U8, name=f"a_bytes{t}", align_bytes=64) for t in range(TILES)]
-        for r in range(PACK):
+        for r in range(2):
+            plane_bf = sb.tile([P, T], BF16, name=f"plane_bf{r}", align_bytes=64)
+            nc.scalar.activation(plane_bf[:], planes[r][:], ACT.Copy)
+            for t in range(TILES):
+                nc.scalar.activation(a_bf[t][:, :, r], plane_bf[:].indirect(offs_t[:, t * LIST_COLS : (t + 1) * LIST_COLS]), ACT.Copy)
+        for r in range(2, PACK):
             for t in range(TILES):
                 nc.vector.tensor_copy(a_bf[t][:, :, r], planes[r][:].indirect(offs_t[:, t * LIST_COLS : (t + 1) * LIST_COLS]))
-        neg_greed = sb.tile([P, TILES], F32, name="neg_greed")
-        nc.gpsimd.tensor_scalar(neg_greed[:], greed_t[:], -1.0, 0.0, ALU.mult, ALU.add)
         scores = [ps.tile([P, J], F32, name=f"scores{t}") for t in range(TILES)]
         for t in range(TILES):
             nc.vector.quantize_mx(out=a_words[t][:].bitcast(FP8X4), scales=a_bytes[t][:], in_=a_bf[t][:].rearrange("p c r -> p (c r)"))
@@ -80,25 +84,26 @@ def tile_attend_bpaircost_kernel(tc, taba, tabb_words, tabb_scales, cost, greed,
         neg_k = sb.tile([P, TILES], F32, name="neg_k")
         k_rz = sb.tile([P, TILES], F32, name="k_rz")
         p = [sb.tile([P, J], F32, name=f"p{t}") for t in range(TILES)]
-        neg_w = [sb.tile([P, J], F32, name=f"neg_w{t}") for t in range(TILES)]
+        wgt = [sb.tile([P, J], F32, name=f"wgt{t}") for t in range(TILES)]
         neg_pw = [sb.tile([P, J], F32, name=f"neg_pw{t}") for t in range(TILES)]
         neg_sum = [sb.tile([P, 1], F32, name=f"neg_sum{t}") for t in range(TILES)]
         p_gain = [sb.tile([P, 1], F32, name=f"p_gain{t}") for t in range(TILES)]
         part = [sb.tile([P, J], F32, name=f"part{t}") for t in range(TILES)]
-        res = [sb.tile([P, J], F32, name=f"res{t}") for t in range(TILES)]
 
         for t in range(TILES):
             nc.vector.tensor_reduce(neg_max[t][:], scores[t][:], AX.X, ALU.max, negate=True)
-        for t in range(TILES):
+            nc.vector.scalar_tensor_tensor(wgt[t][:], scores[t][:], greed_t[:, t : t + 1], cost_t[t][:], ALU.mult, ALU.add)
             nc.scalar.activation(p[t][:], scores[t][:], ACT.Exp, bias=neg_max[t][:], scale=1.0, accum_out=z[:, t : t + 1])
-        for t in range(TILES):
-            nc.vector.scalar_tensor_tensor(neg_w[t][:], scores[t][:], neg_greed[:, t : t + 1], cost_t[t][:], ALU.mult, ALU.subtract)
+        nc.vector.scalar_tensor_tensor(neg_pw[0][:], p[0][:], -1.0, wgt[0][:], ALU.mult, ALU.mult, accum_out=neg_sum[0][:])
         nc.vector.reciprocal(rz[:], z[:])
         nc.scalar.activation(neg_k[:], rz[:], ACT.Copy, scale=-GAIN)
         nc.scalar.activation(k_rz[:], rz[:], ACT.Square, scale=16.0)
+        nc.vector.scalar_tensor_tensor(neg_pw[1][:], p[1][:], -1.0, wgt[1][:], ALU.mult, ALU.mult, accum_out=neg_sum[1][:])
         for t in range(TILES):
-            nc.vector.scalar_tensor_tensor(neg_pw[t][:], p[t][:], 1.0, neg_w[t][:], ALU.mult, ALU.mult, accum_out=neg_sum[t][:])
             nc.scalar.activation(p_gain[t][:], neg_sum[t][:], ACT.Copy, scale=k_rz[:, t : t + 1])
+        for t in range(TILES):
             nc.vector.scalar_tensor_tensor(part[t][:], neg_pw[t][:], neg_k[:, t : t + 1], old_t[t][:], ALU.mult, ALU.add)
-            nc.vector.scalar_tensor_tensor(res[t][:], p[t][:], p_gain[t][:], part[t][:], ALU.mult, ALU.add)
-            nc.sync.dma_start(out[t * P : (t + 1) * P, :], res[t][:])
+        for t, c0, c1 in ((0, 0, J), (1, 0, J // 2), (1, J // 2, J)):
+            res = sb.tile([P, c1 - c0], F32, name=f"res{t}_{c0}")
+            nc.vector.scalar_tensor_tensor(res[:], p[t][:, c0:c1], p_gain[t][:], part[t][:, c0:c1], ALU.mult, ALU.add)
+            nc.sync.dma_start(out[t * P : (t + 1) * P, c0:c1], res[:])

@@ -88,12 +88,12 @@ def tile_attend_bpaircost_kernel(tc, taba, tabb_words, tabb_scales, cost, greed,
         neg_pw = [sb.tile([P, J], F32, name=f"neg_pw{t}") for t in range(TILES)]
         neg_sum = [sb.tile([P, 1], F32, name=f"neg_sum{t}") for t in range(TILES)]
         p_gain = [sb.tile([P, 1], F32, name=f"p_gain{t}") for t in range(TILES)]
-        part = [sb.tile([P, J], F32, name=f"part{t}") for t in range(TILES)]
 
         for t in range(TILES):
-            nc.vector.tensor_reduce(neg_max[t][:], scores[t][:], AX.X, ALU.max, negate=True)
+            neg_s = sb.tile([P, J], F32, name=f"neg_s{t}")
+            nc.vector.tensor_scalar(neg_s[:], scores[t][:], -1.0, None, ALU.mult, ALU.min, accum_out=neg_max[t][:])
             nc.vector.scalar_tensor_tensor(wgt[t][:], scores[t][:], greed_t[:, t : t + 1], cost_t[t][:], ALU.mult, ALU.add)
-            nc.scalar.activation(p[t][:], scores[t][:], ACT.Exp, bias=neg_max[t][:], scale=1.0, accum_out=z[:, t : t + 1])
+            nc.scalar.activation(p[t][:], neg_s[:], ACT.Exp, bias=neg_max[t][:], scale=-1.0, accum_out=z[:, t : t + 1])
         nc.vector.scalar_tensor_tensor(neg_pw[0][:], p[0][:], -1.0, wgt[0][:], ALU.mult, ALU.mult, accum_out=neg_sum[0][:])
         nc.vector.reciprocal(rz[:], z[:])
         nc.scalar.activation(neg_k[:], rz[:], ACT.Copy, scale=-GAIN)
@@ -101,9 +101,20 @@ def tile_attend_bpaircost_kernel(tc, taba, tabb_words, tabb_scales, cost, greed,
         nc.vector.scalar_tensor_tensor(neg_pw[1][:], p[1][:], -1.0, wgt[1][:], ALU.mult, ALU.mult, accum_out=neg_sum[1][:])
         for t in range(TILES):
             nc.scalar.activation(p_gain[t][:], neg_sum[t][:], ACT.Copy, scale=k_rz[:, t : t + 1])
-        for t in range(TILES):
-            nc.vector.scalar_tensor_tensor(part[t][:], neg_pw[t][:], neg_k[:, t : t + 1], old_t[t][:], ALU.mult, ALU.add)
-        for t, c0, c1 in ((0, 0, J), (1, 0, J // 2), (1, J // 2, J)):
+        def add_old(t, c0, c1):
+            part = sb.tile([P, c1 - c0], F32, name=f"part{t}_{c0}")
+            nc.vector.scalar_tensor_tensor(part[:], neg_pw[t][:, c0:c1], neg_k[:, t : t + 1], old_t[t][:, c0:c1], ALU.mult, ALU.add)
+            return part
+
+        def finish(t, c0, c1, part):
             res = sb.tile([P, c1 - c0], F32, name=f"res{t}_{c0}")
-            nc.vector.scalar_tensor_tensor(res[:], p[t][:, c0:c1], p_gain[t][:], part[t][:, c0:c1], ALU.mult, ALU.add)
+            nc.vector.scalar_tensor_tensor(res[:], p[t][:, c0:c1], p_gain[t][:], part[:], ALU.mult, ALU.add)
             nc.sync.dma_start(out[t * P : (t + 1) * P, c0:c1], res[:])
+
+        half = J // 2
+        part0 = add_old(0, 0, J)
+        part1a = add_old(1, 0, half)
+        finish(0, 0, J, part0)
+        part1b = add_old(1, half, J)
+        finish(1, 0, half, part1a)
+        finish(1, half, J, part1b)

from contextlib import ExitStack

import concourse.mybir as mybir

D, T, U, I, J = 512, 1024, 1024, 256, 512
FLOPS = 2 * D * I * J

F32 = mybir.dt.float32
BF16 = mybir.dt.bfloat16
I32 = mybir.dt.int32
U32 = mybir.dt.uint32
U16 = mybir.dt.uint16
U8 = mybir.dt.uint8
FP8X4 = mybir.dt.float8_e4m3fn_x4
ALU = mybir.AluOpType
ACT = mybir.ActivationFunctionType
AX = mybir.AxisListType

P = 128
PACK = 4
TILES = I // P
LIST_COLS = P // 16
GAIN = 256.0


def tile_attend_bpaircost_kernel(tc, taba, tabb_words, tabb_scales, cost, greed, old, offs, offs2, out):
    nc = tc.nc
    with ExitStack() as ctx:
        sb = ctx.enter_context(tc.tile_pool(name="sb", bufs=1))
        ps = ctx.enter_context(tc.psum_pool(name="ps", bufs=1))

        offs_t = sb.tile([P, I // 16], U16, name="offs_t")
        offs2_t = sb.tile([P, J // 16], U16, name="offs2_t")
        b_words = sb.tile([P, U], U32, name="b_words", align_bytes=64)
        b_bytes = sb.tile([P, U], U8, name="b_bytes", align_bytes=64)
        planes = [sb.tile([P, T], F32, name=f"plane{r}", align_bytes=64) for r in range(PACK)]
        greed_t = sb.tile([P, TILES], F32, name="greed_t")
        cost_t = [sb.tile([P, J], F32, name=f"cost{t}") for t in range(TILES)]
        old_t = [sb.tile([P, J], F32, name=f"old{t}") for t in range(TILES)]

        rows = taba.rearrange("(p r) c -> p r c", r=PACK)
        nc.vector.memset(b_bytes[:].bitcast(I32), 0)
        nc.sync.dma_start(offs_t[:], offs)
        nc.sync.dma_start(planes[0][:], rows[:, 0, :])
        nc.sync.dma_start(offs2_t[:], offs2)
        nc.sync.dma_start(b_words[:].bitcast(I32), tabb_words[0].rearrange("p c r -> p (c r)").bitcast(I32))
        for q in range(4):
            nc.sync.dma_start(b_bytes[32 * q : 32 * q + 4, :].bitcast(I32), tabb_scales[0, 4 * q : 4 * q + 4, :].bitcast(I32))
        for r in range(1, PACK):
            nc.sync.dma_start(planes[r][:], rows[:, r, :])
        with nc.allow_non_contiguous_dma(reason="one greed value for each row"):
            nc.sync.dma_start(greed_t[:], greed.rearrange("(t p) o -> p (t o)", p=P))
        for t in range(TILES):
            nc.sync.dma_start(cost_t[t][:], cost[t * P : (t + 1) * P, :])
        for t in range(TILES):
            nc.sync.dma_start(old_t[t][:], old[t * P : (t + 1) * P, :])

        g_words = sb.tile([P, J], U32, name="g_words", align_bytes=64)
        g_bytes = sb.tile([P, J], U8, name="g_bytes", align_bytes=64)
        nc.vector.tensor_copy(g_words[:], b_words[:].indirect(offs2_t[:]))
        nc.vector.tensor_copy(g_bytes[:], b_bytes[:].indirect(offs2_t[:]))

        a_bf = [sb.tile([P, P, PACK], BF16, name=f"a_bf{t}", align_bytes=64) for t in range(TILES)]
        a_words = [sb.tile([P, P], U32, name=f"a_words{t}", align_bytes=64) for t in range(TILES)]
        a_bytes = [sb.tile([P, P], U8, name=f"a_bytes{t}", align_bytes=64) for t in range(TILES)]
        for r in range(2):
            plane_bf = sb.tile([P, T], BF16, name=f"plane_bf{r}", align_bytes=64)
            nc.scalar.activation(plane_bf[:], planes[r][:], ACT.Copy)
            for t in range(TILES):
                nc.scalar.activation(a_bf[t][:, :, r], plane_bf[:].indirect(offs_t[:, t * LIST_COLS : (t + 1) * LIST_COLS]), ACT.Copy)
        for r in range(2, PACK):
            for t in range(TILES):
                nc.vector.tensor_copy(a_bf[t][:, :, r], planes[r][:].indirect(offs_t[:, t * LIST_COLS : (t + 1) * LIST_COLS]))
        scores = [ps.tile([P, J], F32, name=f"scores{t}") for t in range(TILES)]
        for t in range(TILES):
            nc.vector.quantize_mx(out=a_words[t][:].bitcast(FP8X4), scales=a_bytes[t][:], in_=a_bf[t][:].rearrange("p c r -> p (c r)"))
        for t in range(TILES):
            nc.tensor.matmul_mx(out=scores[t][:], lhsT=a_words[t][:].bitcast(FP8X4), lhsT_scale=a_bytes[t][:],
                                rhs=g_words[:].bitcast(FP8X4), rhs_scale=g_bytes[:], start=True, stop=True)

        neg_max = [sb.tile([P, 1], F32, name=f"neg_max{t}") for t in range(TILES)]
        z = sb.tile([P, TILES], F32, name="z")
        rz = sb.tile([P, TILES], F32, name="rz")
        neg_k = sb.tile([P, TILES], F32, name="neg_k")
        k_rz = sb.tile([P, TILES], F32, name="k_rz")
        p = [sb.tile([P, J], F32, name=f"p{t}") for t in range(TILES)]
        wgt = [sb.tile([P, J], F32, name=f"wgt{t}") for t in range(TILES)]
        neg_pw = [sb.tile([P, J], F32, name=f"neg_pw{t}") for t in range(TILES)]
        neg_sum = [sb.tile([P, 1], F32, name=f"neg_sum{t}") for t in range(TILES)]
        p_gain = [sb.tile([P, 1], F32, name=f"p_gain{t}") for t in range(TILES)]

        for t in range(TILES):
            neg_s = sb.tile([P, J], F32, name=f"neg_s{t}")
            nc.vector.tensor_scalar(neg_s[:], scores[t][:], -1.0, None, ALU.mult, ALU.min, accum_out=neg_max[t][:])
            nc.vector.scalar_tensor_tensor(wgt[t][:], scores[t][:], greed_t[:, t : t + 1], cost_t[t][:], ALU.mult, ALU.add)
            nc.scalar.activation(p[t][:], neg_s[:], ACT.Exp, bias=neg_max[t][:], scale=-1.0, accum_out=z[:, t : t + 1])
        nc.vector.scalar_tensor_tensor(neg_pw[0][:], p[0][:], -1.0, wgt[0][:], ALU.mult, ALU.mult, accum_out=neg_sum[0][:])
        nc.vector.reciprocal(rz[:], z[:])
        nc.scalar.activation(neg_k[:], rz[:], ACT.Copy, scale=-GAIN)
        nc.scalar.activation(k_rz[:], rz[:], ACT.Square, scale=16.0)
        nc.vector.scalar_tensor_tensor(neg_pw[1][:], p[1][:], -1.0, wgt[1][:], ALU.mult, ALU.mult, accum_out=neg_sum[1][:])
        for t in range(TILES):
            nc.scalar.activation(p_gain[t][:], neg_sum[t][:], ACT.Copy, scale=k_rz[:, t : t + 1])
        def add_old(t, c0, c1):
            part = sb.tile([P, c1 - c0], F32, name=f"part{t}_{c0}")
            nc.vector.scalar_tensor_tensor(part[:], neg_pw[t][:, c0:c1], neg_k[:, t : t + 1], old_t[t][:, c0:c1], ALU.mult, ALU.add)
            return part

        def finish(t, c0, c1, part):
            res = sb.tile([P, c1 - c0], F32, name=f"res{t}_{c0}")
            nc.vector.scalar_tensor_tensor(res[:], p[t][:, c0:c1], p_gain[t][:], part[:], ALU.mult, ALU.add)
            nc.sync.dma_start(out[t * P : (t + 1) * P, c0:c1], res[:])

        half = J // 2
        part0 = add_old(0, 0, J)
        part1a = add_old(1, 0, half)
        finish(0, 0, J, part0)
        part1b = add_old(1, half, J)
        finish(1, 0, half, part1a)
        finish(1, half, J, part1b)
